import numpy as np
CORES = [24,25,26,27,28,29,30,31,224,225,226,227,228,229,230,231]
N = 16
R, W, B, K = 4096, 128, 128, 8
T = B * K
CAPP = 256
def entries(a): return a.T.reshape(-1)
def pack(v, P): return np.ascontiguousarray(np.asarray(v, np.int32).reshape(-1, P).T)
def lists(rng, how):
    I = rng.integers(0, N * R, (N, T))
    O = np.stack([rng.permutation(np.repeat(np.arange(N), CAPP))[:T] for r in range(N)])
    if how == "full": O = np.stack([rng.permutation(np.repeat(rng.permutation(N)[:T // CAPP], CAPP)) for r in range(N)])
    I = R * O + rng.integers(0, R, (N, T))
    if how == "alike": I = R * O + rng.integers(0, R, (N, 1))
    if how == "edge": I = R * O + np.where(rng.random((N, T)) < 0.5, 0, R - 1)
    if how == "sorted": I = np.sort(I, axis=1)
    return {"idx": np.stack([pack(I[r], 128) for r in range(N)])}
def setup_inputs(rng):
    return dict({"tab": rng.standard_normal((N, R, W), dtype=np.float32)}, **lists(rng, "uniform"))
def setup_inputs_alike(rng):
    d = setup_inputs(rng); d.update(lists(rng, "alike"))
    for k in ("tab",): d[k] = (d[k].astype(np.float32) * 1024.0).astype(d[k].dtype)
    return d
def setup_inputs_edge(rng):
    d = setup_inputs(rng); d.update(lists(rng, "edge"))
    for k in ("tab",): d[k] = (d[k].astype(np.float32) * (1 / 1024.0)).astype(d[k].dtype)
    return d
def setup_inputs_full(rng):
    d = setup_inputs(rng); d.update(lists(rng, "full"))
    return d
def setup_inputs_sorted(rng):
    d = setup_inputs(rng); d.update(lists(rng, "sorted"))
    return d
def check_inputs(x):
    bad = []
    if x["idx"].min() < 0 or x["idx"].max() >= N * R: bad.append("idx out of range")
    if max(int(np.bincount(entries(a) // R, minlength=N).max()) for a in x["idx"]) > CAPP: bad.append("more than CAPP entries of a list point into one rank's part")
    return bad
def reference(tab, idx):
    A = np.concatenate(list(tab), axis=0).astype(np.float64)
    return {"y": np.stack([A[entries(idx[r])].reshape(B, K, W).sum(axis=1) for r in range(N)]).astype(np.float32)}

@@ -1,0 +1,390 @@
+from concourse.bass import DstId, RemoteDMATransfer
+from concourse.mybir import AluOpType, ActivationFunctionType
+
+N = 16
+F32, BF, I32, U16 = "float32", "bfloat16", "int32", "uint16"
+SCRATCH = {
+    "IDX": ("sbuf", [128, 8], I32), "IT": ("sbuf", [128, 64], I32), "FT": ("sbuf", [128, 128], F32),
+    "ONESF": ("sbuf", [128, 128], F32), "IDENT": ("sbuf", [128, 128], F32), "ONESB": ("sbuf", [128, 128], BF),
+    "LT": ("sbuf", [128, 128], BF), "CLT": ("sbuf", [128, 128], BF), "AT": ("sbuf", [128, 128], BF),
+    "IOTAB": ("sbuf", [128, 128], BF), "EXP": ("sbuf", [128, 1024], BF), "BSEL": ("sbuf", [128, 128], BF),
+    "CW": ("sbuf", [128, 2], F32),
+    "OH": ("sbuf", [128, 128], BF), "TOTB": ("sbuf", [128, 128], BF), "SELM": ("sbuf", [128, 128], F32),
+    "TR": ("sbuf", [128, 128], F32), "LH": ("sbuf", [128, 1024], BF), "RH": ("sbuf", [128, 512], BF),
+    "MSG": ("sbuf", [128, 256], BF), "LAND": ("sbuf", [128, 256], BF), "RELAY": ("sbuf", [128, 128], BF),
+    "HL": ("sbuf", [128, 64], BF), "TM": ("sbuf", [128, 256], F32), "TS": ("sbuf", [128, 256], F32),
+    "U1": ("sbuf", [128, 256], U16), "UF": ("sbuf", [128, 256], U16), "U2": ("sbuf", [128, 256], U16),
+    "FL": ("sbuf", [128, 4097], F32), "G": ("sbuf", [128, 4096], F32), "SC": ("sbuf", [128, 4112], F32),
+    "P": ("sbuf", [128, 2048], F32), "AGG": ("sbuf", [128, 2048], F32), "RECV": ("sbuf", [128, 1024], F32),
+    "RX": ("sbuf", [128, 128], F32), "YS": ("sbuf", [128, 128], F32),
+    "TABN": ("sbuf", [128, 4096], F32), "TABT": ("sbuf", [128, 4096], F32),
+    "TP0": ("psum", [128, 512], F32), "TP1": ("psum", [128, 512], F32), "TP2": ("psum", [128, 512], F32),
+    "TP3": ("psum", [128, 512], F32), "PB4": ("psum", [128, 512], F32), "PB5": ("psum", [128, 512], F32),
+    "PB6": ("psum", [128, 512], F32), "PB7": ("psum", [128, 512], F32),
+}
+SEMAPHORES = (["vs", "ss", "ps", "gs", "ix", "ll", "lr", "rl", "snt", "ag0", "ag1", "rx", "yd"]
+              + ["td%d" % q for q in range(8)] + ["rc%d" % q for q in range(8)])
+
+
+def _engines(m):
+    out, b = [], 1
+    while b <= m:
+        if m & b:
+            out.append(b)
+        b <<= 1
+    return out
+
+
+def _pow2(n):
+    p = 1
+    while 2 * p <= n:
+        p *= 2
+    return p
+
+
+def rank_program(g, core, T, topo):
+    me = T.rank_of(core)
+    if me is None:
+        return
+    A, S = AluOpType, T.sem
+    COPY = ActivationFunctionType.Copy
+    cores = list(T.cores)
+
+    def same_chip(a, b):
+        return topo.host(a) == topo.host(b) and topo.chip(a) == topo.chip(b)
+
+    loc = [r for r in range(N) if same_chip(cores[r], core)]
+    rem = [r for r in range(N) if not same_chip(cores[r], core)]
+    li, nl = loc.index(me), len(loc)
+    lb, rb = 16 * min(loc), 16 * min(rem)
+
+    def ports_of(ranks, others):
+        return [cores[r] for r in ranks if topo.may_write(cores[r], cores[others[0]])]
+
+    def aggmap(ranks, others):
+        ports, m = ports_of(ranks, others), {}
+        for d in sorted(set(topo.die(p) for p in ports)):
+            pd = [p for p in ports if topo.die(p) == d]
+            qd = [r for r in others if topo.die(cores[r]) == d]
+            for i, r in enumerate(qd):
+                m[r] = (pd[i % len(pd)], i // len(pd))
+        return m
+
+    ports = ports_of(loc, rem)
+    is_port = core in ports
+    buddy = {}
+    for d in sorted(set(topo.die(p) for p in ports)):
+        pd = [p for p in ports if topo.die(p) == d]
+        nd = [cores[r] for r in loc if topo.die(cores[r]) == d and cores[r] not in ports]
+        for i, x in enumerate(nd):
+            buddy[x] = pd[i % len(pd)]
+    clients = [x for x in buddy if buddy[x] == core]
+    am = aggmap(loc, rem)
+
+    def did(c):
+        rid, pid = topo.addr(c, core)
+        return DstId(rid=rid, pnc=pid)
+
+    n = {"v": 0, "s": 0, "p": 0, "g": 0, "snt": 0}
+
+    def V(i):
+        i.then_inc(S.vs, 1)
+        n["v"] += 1
+        return n["v"]
+
+    def SA(i):
+        i.then_inc(S.ss, 1)
+        n["s"] += 1
+        return n["s"]
+
+    def PE(i):
+        i.then_inc(S.ps, 1)
+        n["p"] += 1
+        return n["p"]
+
+    def GC(i):
+        i.then_inc(S.gs, 1)
+        n["g"] += 1
+        return n["g"]
+
+    v, pe, sc = g.vector, g.tensor, g.scalar
+
+    def vw():
+        v.wait_ge(S.vs, n["v"])
+
+    def it(k):
+        return T.IT[:, 8 * k:8 * k + 8]
+
+    def ft(k):
+        return T.FT[:, 8 * k:8 * k + 8]
+
+    g.sync.dma_start(T.IDX[:], T.idx[:]).then_inc(S.ix, 16)
+    for q in range(8):
+        (g.sync if q % 2 == 0 else sc).dma_start(T.TABN[:, 512 * q:512 * q + 512],
+                                                 T.tab[512 * q:512 * q + 512, :]).then_inc(S["td%d" % q], 16)
+
+    V(v.memset(T.ONESF[:], 1.0))
+    V(v.memset(T.ONESB[:], 1.0))
+    m1 = V(v.memset(T.AT[:], 256.0))
+    V(v.memset(T.MSG[:], 0.0))
+    V(v.memset(T.BSEL[:], 1.0))
+    V(v.memset(T.CW[:, 0:1], 0.0))
+    V(v.memset(T.CW[:, 1:2], 1.0))
+    V(v.memset(T.FL[:, 0:1], 0.0))
+    V(v.memset(T.SC[:, 0:4112:257], 0.0))
+    m2 = V(v.memset(T.EXP[:], 1.0))
+
+    g.wait_ge(S.vs, m1)
+    g_ident = GC(g.affine_select(T.IDENT[:], T.ONESF[:], [[-1, 128]], A.is_equal, 0.0, 0, 1))
+    g_iota = GC(g.iota(T.IOTAB[:], [[1, 128]], 0, 0, allow_small_or_imprecise_dtypes=True))
+    GC(g.affine_select(T.LT[:], T.ONESB[:], [[1, 128]], A.is_gt, 0.0, 0, -1))
+    GC(g.affine_select(T.AT[:], T.AT[:], [[-1, 128]], A.is_gt, 0.0, 0, 1))
+    g.wait_ge(S.gs, n["g"])
+    GC(g.affine_select(T.CLT[:], T.LT[:], [[-8, 16], [0, 8]], A.is_ge, 0.0, 0, 1))
+    g_rank = GC(g.affine_select(T.AT[:], T.AT[:], [[8, 16], [0, 8]], A.is_ge, 0.0, 7, -1))
+    g.wait_ge(S.vs, m2)
+    GC(g.affine_select(T.BSEL[:], T.BSEL[:], [[0, 8], [-8, 16]], A.is_ge, 0.0, 0, 1))
+    g.wait_ge(S.gs, n["g"])
+    GC(g.affine_select(T.BSEL[:], T.BSEL[:], [[0, 8], [8, 16]], A.is_ge, 0.0, 7, -1))
+    g_exp = GC(g.affine_select(T.EXP[:], T.EXP[:], [[-16, 8], [0, 8], [-1, 16]], A.is_equal, 0.0, 0, 1))
+
+    TP = [T.TP0, T.TP1, T.TP2, T.TP3]
+    evac = {}
+    nxt = [0]
+
+    def tiles(upto):
+        while nxt[0] <= upto:
+            k = nxt[0]
+            nxt[0] += 1
+            q, t = k // 4, k % 4
+            if k == 0:
+                pe.wait_ge(S.gs, g_ident)
+            if t == 0:
+                pe.wait_ge(S["td%d" % q], 16)
+                if q >= 4:
+                    pe.wait_ge(S.ss, evac[q - 4])
+            c = PE(pe.transpose(TP[q % 4][:, 128 * t:128 * t + 128], T.TABN[:, 128 * k:128 * k + 128], T.IDENT[:]))
+            if t == 3:
+                sc.wait_ge(S.ps, c)
+                for u in range(4):
+                    evac[q] = SA(sc.activation(T.TABT[:, 512 * q + u:512 * q + 512:4], TP[q % 4][:, 128 * u:128 * u + 128], COPY))
+
+    tiles(0)
+    OWNI, HII, LOI, VPI, RKI, R7I = it(0), it(1), it(2), it(3), it(4), it(5)
+    OWNF, OWN2, HIF, LOF, VP, NLF, ISL, NL4, RKF, R7F, HV, IHF, RK1, COLF, V2F = [ft(k) for k in range(15)]
+    v.wait_ge(S.ix, 16)
+    V(v.tensor_scalar(OWNI, T.IDX[:], 12, None, A.logical_shift_right))
+    V(v.tensor_scalar(HII, T.IDX[:], 4032, None, A.bitwise_and))
+    V(v.tensor_scalar(LOI, T.IDX[:], 63, None, A.bitwise_and))
+    vw()
+    V(v.tensor_copy(OWNF, OWNI))
+    vw()
+    v.wait_ge(S.gs, g_iota)
+    for c in range(8):
+        oh = V(v.tensor_scalar(T.OH[:, c:128:8], T.IOTAB[:, 0:16], OWNF[:, c:c + 1], None, A.is_equal))
+    V(v.tensor_copy(HIF, HII))
+    V(v.tensor_copy(LOF, LOI))
+    V(v.tensor_scalar(OWN2, OWNF, 2.0, None, A.mult))
+    pe.wait_ge(S.vs, oh)
+    c = PE(pe.matmul(T.PB4[:, 0:128], T.OH[:], T.ONESB[:], True, True))
+    tiles(1)
+    v.wait_ge(S.ps, c)
+    c = V(v.tensor_copy(T.TOTB[:], T.PB4[:, 0:128]))
+    pe.wait_ge(S.vs, c)
+    pe.wait_ge(S.gs, g_rank)
+    pe.matmul(T.PB5[:, 0:128], T.LT[:], T.OH[:], True, False)
+    pe.matmul(T.PB5[:, 0:128], T.AT[:], T.OH[:], False, False)
+    c = PE(pe.matmul(T.PB5[:, 0:128], T.TOTB[:], T.CLT[:], False, True))
+    tiles(5)
+    v.wait_ge(S.ps, c)
+    V(v.tensor_tensor(T.SELM[:], T.PB5[:, 0:128], T.OH[:], A.mult))
+    vw()
+    V(v.tensor_tensor(T.TR[:, 0:64], T.SELM[:, 0:64], T.SELM[:, 64:128], A.add))
+    vw()
+    V(v.tensor_tensor(T.TR[:, 64:96], T.TR[:, 0:32], T.TR[:, 32:64], A.add))
+    vw()
+    V(v.tensor_tensor(T.TR[:, 96:112], T.TR[:, 64:80], T.TR[:, 80:96], A.add))
+    vw()
+    V(v.tensor_tensor(VP, T.TR[:, 96:104], T.TR[:, 104:112], A.add))
+    vw()
+    V(v.tensor_copy(VPI, VP))
+    V(v.tensor_scalar(NLF, VP, 256.0, None, A.is_ge))
+    V(v.tensor_scalar(ISL, VP, 256.0, None, A.is_lt))
+    vw()
+    V(v.tensor_scalar(RKI, VPI, 255, None, A.bitwise_and))
+    V(v.tensor_scalar(R7I, VPI, 127, None, A.bitwise_and))
+    V(v.tensor_scalar(NL4, NLF, 4096.0, None, A.mult))
+    vw()
+    V(v.tensor_copy(RKF, RKI))
+    V(v.tensor_copy(R7F, R7I))
+    V(v.tensor_tensor(HV, NL4, HIF, A.add))
+    vw()
+    V(v.tensor_scalar(IHF, RKF, 128.0, None, A.is_ge))
+    V(v.tensor_scalar(RK1, RKF, 1.0, None, A.add))
+    vw()
+    V(v.tensor_tensor(COLF, IHF, OWN2, A.add))
+    V(v.tensor_tensor(V2F, RK1, ISL, A.mult))
+    vw()
+    for c in range(8):
+        V(v.tensor_scalar(T.LH[:, 128 * c:128 * c + 128], T.IOTAB[:], R7F[:, c:c + 1], None, A.is_equal))
+        V(v.tensor_scalar(T.RH[:, 64 * c:64 * c + 32], T.IOTAB[:, 0:32], COLF[:, c:c + 1], HV[:, c:c + 1], A.is_equal, A.mult))
+        k = V(v.tensor_scalar(T.RH[:, 64 * c + 32:64 * c + 64], T.IOTAB[:, 0:32], COLF[:, c:c + 1], LOF[:, c:c + 1], A.is_equal, A.mult))
+        pe.wait_ge(S.vs, k)
+        i = pe.matmul(T.PB4[:, 128:192], T.LH[:, 128 * c:128 * c + 128], T.RH[:, 64 * c:64 * c + 64], c == 0, c == 7)
+        if c == 7:
+            k = PE(i)
+        tiles(6 + c)
+    for c in range(8):
+        V(v.tensor_scalar(T.MSG[:, 4 + c:256:16], T.IOTAB[:, 0:16], OWNF[:, c:c + 1], V2F[:, c:c + 1], A.is_equal, A.mult))
+    v.wait_ge(S.ps, k)
+    for s in range(2):
+        for ih in range(2):
+            V(v.tensor_copy(T.MSG[:, 2 * s + ih:256:16], T.PB4[:, 128 + 32 * s + ih:128 + 32 * s + 32:2]))
+    msg = n["v"]
+    vw()
+    V(v.tensor_copy(T.LAND[:, 16 * me:16 * me + 16], T.MSG[:, 16 * me:16 * me + 16]))
+
+    def fused(trs):
+        g.remote_dma_fused(trs, local_sem=S.snt)
+
+    def group(engs, i, per):
+        return sum(engs[i * per:(i + 1) * per])
+
+    eng_on = _engines(topo.mask(core, cores[loc[(li + 1) % nl]]))
+    eng_off = _engines(topo.mask(ports[0], cores[rem[0]]))
+    per_l, per_r = _pow2(len(eng_on) // (nl - 1)), _pow2(len(eng_off) // len(rem))
+
+    def cross(src, r):
+        fused([RemoteDMATransfer(dst_ids=[did(cores[o])], dma_engine_mask=group(eng_off, j, per_r), remote_sem=S.lr,
+                                 src=src[:, 16 * j:16 * j + 16], dst=T.LAND[:, 16 * r:16 * r + 16]) for j, o in enumerate(rem)])
+        n["snt"] += per_r * len(rem)
+
+    g.wait_ge(S.vs, msg)
+    if is_port:
+        cross(T.MSG[:, rb:rb + 128], me)
+    else:
+        rid, pid = topo.addr(buddy[core], core)
+        g.remote_dma(T.RELAY[:], T.MSG[:, rb:rb + 128], S.rl, S.snt, pid, rid, topo.mask(core, buddy[core]))
+        n["snt"] += len(eng_on)
+    others = [r for r in loc if r != me]
+    fused([RemoteDMATransfer(dst_ids=[did(cores[o])], dma_engine_mask=group(eng_on, j, per_l), remote_sem=S.ll,
+                             src=T.MSG[:, 16 * o:16 * o + 16], dst=T.LAND[:, 16 * me:16 * me + 16]) for j, o in enumerate(others)])
+    n["snt"] += per_l * len(others)
+    for x in clients:
+        g.wait_ge(S.rl, len(eng_on) * len(clients))
+        cross(T.RELAY[:], T.rank_of(x))
+
+    ready = {}
+
+    def expand(cb, hh, sem, cnt):
+        v.wait_ge(sem, cnt)
+        vw()
+        for s in range(2):
+            for ih in range(2):
+                k = V(v.tensor_copy(T.HL[:, 32 * hh + 16 * s + ih:32 * hh + 16 * s + 16:2], T.LAND[:, cb + 2 * s + ih:cb + 128:16]))
+        pe.wait_ge(S.vs, k)
+        pe.wait_ge(S.gs, g_exp)
+        for x in range(8):
+            pe.matmul(T.PB6[:, cb + x:cb + 128:8], T.EXP[:, 128 * x:128 * x + 128], T.HL[:, 32 * hh:32 * hh + 16], True, False)
+            PE(pe.matmul(T.PB6[:, cb + x:cb + 128:8], T.EXP[:, 128 * x:128 * x + 128], T.HL[:, 32 * hh + 16:32 * hh + 32], False, True))
+        k = PE(pe.matmul(T.PB7[:, cb:cb + 128], T.BSEL[:], T.LAND[:, cb:cb + 128], True, True))
+        v.wait_ge(S.ps, k)
+        V(v.tensor_scalar(T.UF[:, cb:cb + 128], T.PB6[:, cb:cb + 128], 4096.0, None, A.is_ge))
+        V(v.tensor_scalar(T.TM[:, cb:cb + 128], T.PB6[:, cb:cb + 128], 4096.0, -4096.0, A.is_ge, A.mult))
+        V(v.tensor_copy(T.U2[:, cb:cb + 128], T.PB7[:, cb:cb + 128]))
+        vw()
+        V(v.tensor_tensor(T.TS[:, cb:cb + 128], T.PB6[:, cb:cb + 128], T.TM[:, cb:cb + 128], A.add))
+        vw()
+        ready[cb] = V(v.tensor_copy(T.U1[:, cb:cb + 128], T.TS[:, cb:cb + 128]))
+        V(v.tensor_copy(T.FL[:, 1 + 16 * cb:1 + 16 * cb + 2048], T.CW[:, 0:2].indirect(T.UF[:, cb:cb + 128])))
+
+    tiles(18)
+    expand(lb, 0, S.ll, per_l * (nl - 1))
+    tiles(25)
+    pe.wait_ge(S.vs, ready[lb])
+    expand(rb, 1, S.lr, per_r * len(rem))
+    tiles(31)
+
+    slot0 = [r for r in rem if am[r][1] == 0]
+    slot1 = [r for r in rem if am[r][1] == 1]
+    lord = [loc[(li + d) % nl] for d in range(1, nl)]
+    order = slot0 + slot1 + lord + [me]
+    sc.wait_ge(S.ss, n["s"])
+    sc.wait_ge(S.vs, ready[rb])
+    gd = {}
+    for r in order:
+        gd[r] = SA(sc.activation(T.G[:, 256 * r:256 * r + 256], T.TABT[:, 0:4096].indirect(T.U1[:, 16 * r:16 * r + 16]), COPY))
+    vw()
+    sd, pd = {}, {}
+
+    def ends(r):
+        v.wait_ge(S.vs, sd[r])
+        pd[r] = V(v.tensor_copy(T.P[:, 128 * r:128 * r + 128],
+                                T.SC[:, 257 * r:257 * r + 257].indirect(T.U2[:, 16 * r + 4:16 * r + 12])))
+
+    for j, r in enumerate(order):
+        v.wait_ge(S.ss, gd[r])
+        sd[r] = V(v.tensor_tensor_scan(T.SC[:, 257 * r + 1:257 * r + 257], T.FL[:, 256 * r:256 * r + 256],
+                                       T.G[:, 256 * r:256 * r + 256], 0.0, A.mult, A.add))
+        if j:
+            ends(order[j - 1])
+    ends(order[-1])
+
+    per_p = _pow2(len(eng_on) // 4)
+
+    def to_agg(rs):
+        g.wait_ge(S.vs, pd[rs[-1]])
+        trs = [RemoteDMATransfer(dst_ids=[did(am[r][0])], dma_engine_mask=group(eng_on, j, per_p), remote_sem=S["ag%d" % am[r][1]],
+                                 src=T.P[:, 128 * r:128 * r + 128],
+                                 dst=T.AGG[:, 128 * (8 * am[r][1] + li):128 * (8 * am[r][1] + li) + 128])
+               for j, r in enumerate(rs) if am[r][0] != core]
+        fused(trs)
+        n["snt"] += per_p * len(trs)
+
+    def to_req(rs):
+        g.wait_ge(S.vs, pd[rs[-1]])
+        fused([RemoteDMATransfer(dst_ids=[did(cores[r])], dma_engine_mask=group(eng_on, j, per_p), remote_sem=S["rc%d" % li],
+                                 src=T.P[:, 128 * r:128 * r + 128], dst=T.RECV[:, 128 * li:128 * li + 128]) for j, r in enumerate(rs)])
+        n["snt"] += per_p * len(rs)
+
+    def fold(s):
+        for r in rem:
+            if am[r] == (core, s):
+                g.wait_ge(S["ag%d" % s], per_p * (nl - 1))
+                srcs = [T.AGG[:, 128 * (8 * s + j):128 * (8 * s + j) + 128] for j in range(nl) if j != li]
+                fused([RemoteDMATransfer(dst_ids=[did(cores[r])], dma_engine_mask=sum(eng_off), remote_sem=S.rx,
+                                         srcs=srcs + [T.P[:, 128 * r:128 * r + 128]], dsts=[T.RX[:]], alu_op=1)])
+                n["snt"] += len(eng_off)
+
+    to_agg(slot0)
+    to_agg(slot1)
+    fold(0)
+    to_req(lord[0:4])
+    fold(1)
+    to_req(lord[4:])
+
+    pe.wait_ge(S.ss, evac[4])
+    seq = [(li - d) % nl for d in range(1, 5)] + [-1] + [(li - d) % nl for d in range(5, nl)] + [-2]
+    for j, s in enumerate(seq):
+        if s == -1:
+            pe.wait_ge(S.vs, pd[me])
+            src = T.P[:, 128 * me:128 * me + 128]
+        elif s == -2:
+            pe.wait_ge(S.rx, len(eng_off))
+            src = T.RX[:]
+        else:
+            pe.wait_ge(S["rc%d" % s], per_p)
+            src = T.RECV[:, 128 * s:128 * s + 128]
+        i = pe.matmul(T.TP0[:, 0:128], src, T.IDENT[:], j == 0, j == len(seq) - 1)
+    k = PE(i)
+    v.wait_ge(S.ps, k)
+    k = V(v.tensor_copy(T.YS[:], T.TP0[:, 0:128]))
+    g.sync.wait_ge(S.vs, k)
+    g.sync.dma_start(T.y[:], T.YS[:]).then_inc(S.yd, 16)
+
+    g.wait_ge(S.yd, 16)
+    g.wait_ge(S.vs, n["v"])
+    g.wait_ge(S.ss, n["s"])
+    g.wait_ge(S.ps, n["p"])
+    g.wait_ge(S.gs, n["g"])
+    g.wait_ge(S.snt, n["snt"])

@@ -8,13 +8,13 @@ SCRATCH = {
     "ONESF": ("sbuf", [128, 128], F32), "IDENT": ("sbuf", [128, 128], F32), "ONESB": ("sbuf", [128, 128], BF),
     "LT": ("sbuf", [128, 128], BF), "CLT": ("sbuf", [128, 128], BF), "AT": ("sbuf", [128, 128], BF),
     "IOTAB": ("sbuf", [128, 128], BF), "EXP": ("sbuf", [128, 1024], BF), "BSEL": ("sbuf", [128, 128], BF),
-    "CW": ("sbuf", [128, 2], F32),
+    "SH": ("sbuf", [128, 129], BF), "D": ("sbuf", [128, 4096], BF),
     "OH": ("sbuf", [128, 128], BF), "TOTB": ("sbuf", [128, 128], BF), "SELM": ("sbuf", [128, 128], F32),
     "TR": ("sbuf", [128, 128], F32), "LH": ("sbuf", [128, 1024], BF), "RH": ("sbuf", [128, 512], BF),
     "MSG": ("sbuf", [128, 256], BF), "LAND": ("sbuf", [128, 256], BF), "RELAY": ("sbuf", [128, 128], BF),
     "HL": ("sbuf", [128, 64], BF), "TM": ("sbuf", [128, 256], F32), "TS": ("sbuf", [128, 256], F32),
-    "U1": ("sbuf", [128, 256], U16), "UF": ("sbuf", [128, 256], U16), "U2": ("sbuf", [128, 256], U16),
-    "FL": ("sbuf", [128, 4097], F32), "G": ("sbuf", [128, 4096], F32), "SC": ("sbuf", [128, 4112], F32),
+    "U1": ("sbuf", [128, 256], U16), "U2": ("sbuf", [128, 256], U16),
+    "G": ("sbuf", [128, 4096], F32), "SC": ("sbuf", [128, 4112], F32),
     "P": ("sbuf", [128, 2048], F32), "AGG": ("sbuf", [128, 2048], F32), "RECV": ("sbuf", [128, 1024], F32),
     "RX": ("sbuf", [128, 128], F32), "YS": ("sbuf", [128, 128], F32),
     "TABN": ("sbuf", [128, 4096], F32), "TABT": ("sbuf", [128, 4096], F32),
@@ -23,7 +23,7 @@ SCRATCH = {
     "PB6": ("psum", [128, 512], F32), "PB7": ("psum", [128, 512], F32),
 }
 SEMAPHORES = (["vs", "ss", "ps", "gs", "ix", "ll", "lr", "rl", "snt", "ag0", "ag1", "rx", "yd"]
-              + ["td%d" % q for q in range(8)] + ["rc%d" % q for q in range(8)])
+              + ["ta%d" % q for q in range(4)] + ["td%d" % q for q in range(1, 8)] + ["rc%d" % q for q in range(8)])
 
 
 def _engines(m):
@@ -119,7 +119,10 @@ def rank_program(g, core, T, topo):
         return T.FT[:, 8 * k:8 * k + 8]
 
     g.sync.dma_start(T.IDX[:], T.idx[:]).then_inc(S.ix, 16)
-    for q in range(8):
+    for t in range(4):
+        (sc if t % 2 == 0 else g.sync).dma_start(T.TABN[:, 128 * t:128 * t + 128],
+                                                 T.tab[128 * t:128 * t + 128, :]).then_inc(S["ta%d" % t], 16)
+    for q in range(1, 8):
         (g.sync if q % 2 == 0 else sc).dma_start(T.TABN[:, 512 * q:512 * q + 512],
                                                  T.tab[512 * q:512 * q + 512, :]).then_inc(S["td%d" % q], 16)
 
@@ -128,9 +131,7 @@ def rank_program(g, core, T, topo):
     m1 = V(v.memset(T.AT[:], 256.0))
     V(v.memset(T.MSG[:], 0.0))
     V(v.memset(T.BSEL[:], 1.0))
-    V(v.memset(T.CW[:, 0:1], 0.0))
-    V(v.memset(T.CW[:, 1:2], 1.0))
-    V(v.memset(T.FL[:, 0:1], 0.0))
+    V(v.memset(T.SH[:], 1.0))
     V(v.memset(T.SC[:, 0:4112:257], 0.0))
     m2 = V(v.memset(T.EXP[:], 1.0))
 
@@ -144,6 +145,7 @@ def rank_program(g, core, T, topo):
     g_rank = GC(g.affine_select(T.AT[:], T.AT[:], [[8, 16], [0, 8]], A.is_ge, 0.0, 7, -1))
     g.wait_ge(S.vs, m2)
     GC(g.affine_select(T.BSEL[:], T.BSEL[:], [[0, 8], [-8, 16]], A.is_ge, 0.0, 0, 1))
+    g_sh = GC(g.affine_select(T.SH[:], T.SH[:], [[1, 129]], A.is_equal, 0.0, -1, -1))
     g.wait_ge(S.gs, n["g"])
     GC(g.affine_select(T.BSEL[:], T.BSEL[:], [[0, 8], [8, 16]], A.is_ge, 0.0, 7, -1))
     g_exp = GC(g.affine_select(T.EXP[:], T.EXP[:], [[-16, 8], [0, 8], [-1, 16]], A.is_equal, 0.0, 0, 1))
@@ -159,15 +161,33 @@ def rank_program(g, core, T, topo):
             q, t = k // 4, k % 4
             if k == 0:
                 pe.wait_ge(S.gs, g_ident)
-            if t == 0:
+            if q == 0:
+                pe.wait_ge(S["ta%d" % t], 16)
+            elif t == 0:
                 pe.wait_ge(S["td%d" % q], 16)
-                if q >= 4:
-                    pe.wait_ge(S.ss, evac[q - 4])
-            c = PE(pe.transpose(TP[q % 4][:, 128 * t:128 * t + 128], T.TABN[:, 128 * k:128 * k + 128], T.IDENT[:]))
-            if t == 3:
+            bank, col = TP[q % 4], 128 * t
+            if k >= 30:
+                bank, col = TP[k - 30], 0
+                pe.wait_ge(S.ss, evac[k - 26])
+            elif t == 0 and q >= 4:
+                pe.wait_ge(S.ss, evac[q - 4])
+            c = PE(pe.transpose(bank[:, col:col + 128], T.TABN[:, 128 * k:128 * k + 128], T.IDENT[:]))
+            if q == 0:
+                if t == 3:
+                    sc.wait_ge(S.ps, c)
+                    evac[0] = SA(sc.activation(T.TABT[:, 0:512], T.TP0[:, 0:512], COPY))
+            elif q < 7:
+                if t == 3:
+                    sc.wait_ge(S.ps, c)
+                    for u in range(4):
+                        evac[q] = SA(sc.activation(T.TABT[:, 512 * q + u:512 * q + 512:4], bank[:, 128 * u:128 * u + 128], COPY))
+            elif t == 1:
                 sc.wait_ge(S.ps, c)
-                for u in range(4):
-                    evac[q] = SA(sc.activation(T.TABT[:, 512 * q + u:512 * q + 512:4], TP[q % 4][:, 128 * u:128 * u + 128], COPY))
+                for u in range(2):
+                    SA(sc.activation(T.TABT[:, 512 * q + u:512 * q + 512:4], bank[:, 128 * u:128 * u + 128], COPY))
+            elif t >= 2:
+                sc.wait_ge(S.ps, c)
+                evac[q] = SA(sc.activation(T.TABT[:, 512 * q + t:512 * q + 512:4], bank[:, 0:128], COPY))
 
     tiles(0)
     OWNI, HII, LOI, VPI, RKI, R7I = it(0), it(1), it(2), it(3), it(4), it(5)
@@ -276,7 +296,7 @@ def rank_program(g, core, T, topo):
 
     ready = {}
 
-    def expand(cb, hh, sem, cnt):
+    def expand(cb, hh, ranks, sem, cnt):
         v.wait_ge(sem, cnt)
         vw()
         for s in range(2):
@@ -284,31 +304,47 @@ def rank_program(g, core, T, topo):
                 k = V(v.tensor_copy(T.HL[:, 32 * hh + 16 * s + ih:32 * hh + 16 * s + 16:2], T.LAND[:, cb + 2 * s + ih:cb + 128:16]))
         pe.wait_ge(S.vs, k)
         pe.wait_ge(S.gs, g_exp)
+        pb = 256 * hh
         for x in range(8):
-            pe.matmul(T.PB6[:, cb + x:cb + 128:8], T.EXP[:, 128 * x:128 * x + 128], T.HL[:, 32 * hh:32 * hh + 16], True, False)
-            PE(pe.matmul(T.PB6[:, cb + x:cb + 128:8], T.EXP[:, 128 * x:128 * x + 128], T.HL[:, 32 * hh + 16:32 * hh + 32], False, True))
+            PE(pe.matmul(T.PB6[:, pb + x:pb + 256:8], T.EXP[:, 128 * x:128 * x + 128], T.HL[:, 32 * hh:32 * hh + 32], True, True))
         k = PE(pe.matmul(T.PB7[:, cb:cb + 128], T.BSEL[:], T.LAND[:, cb:cb + 128], True, True))
+        v.wait_ge(S.gs, g_sh)
+        for r in ranks:
+            V(v.tensor_scalar(T.D[:, 256 * r:256 * r + 129], T.SH[:, 0:129], T.LAND[:, 16 * r:16 * r + 1], 4096.0, A.mult, A.is_ge))
+            V(v.tensor_scalar(T.D[:, 256 * r + 129:256 * r + 256], T.SH[:, 1:128], T.LAND[:, 16 * r + 1:16 * r + 2], 4096.0,
+                              A.mult, A.is_ge))
         v.wait_ge(S.ps, k)
-        V(v.tensor_scalar(T.UF[:, cb:cb + 128], T.PB6[:, cb:cb + 128], 4096.0, None, A.is_ge))
-        V(v.tensor_scalar(T.TM[:, cb:cb + 128], T.PB6[:, cb:cb + 128], 4096.0, -4096.0, A.is_ge, A.mult))
+        V(v.tensor_scalar(T.TM[:, cb:cb + 128], T.PB6[:, pb:pb + 128], 4096.0, -4096.0, A.is_ge, A.mult))
         V(v.tensor_copy(T.U2[:, cb:cb + 128], T.PB7[:, cb:cb + 128]))
         vw()
-        V(v.tensor_tensor(T.TS[:, cb:cb + 128], T.PB6[:, cb:cb + 128], T.TM[:, cb:cb + 128], A.add))
+        V(v.tensor_tensor(T.TS[:, cb:cb + 128], T.PB6[:, pb:pb + 128], T.TM[:, cb:cb + 128], A.add))
+        vw()
+        V(v.tensor_tensor(T.TS[:, cb:cb + 128], T.PB6[:, pb + 128:pb + 256], T.TS[:, cb:cb + 128], A.add))
         vw()
         ready[cb] = V(v.tensor_copy(T.U1[:, cb:cb + 128], T.TS[:, cb:cb + 128]))
-        V(v.tensor_copy(T.FL[:, 1 + 16 * cb:1 + 16 * cb + 2048], T.CW[:, 0:2].indirect(T.UF[:, cb:cb + 128])))
 
-    tiles(18)
-    expand(lb, 0, S.ll, per_l * (nl - 1))
-    tiles(25)
+    tiles(21)
+    expand(lb, 0, loc, S.ll, per_l * (nl - 1))
+    tiles(28)
     pe.wait_ge(S.vs, ready[lb])
-    expand(rb, 1, S.lr, per_r * len(rem))
+    expand(rb, 1, rem, S.lr, per_r * len(rem))
     tiles(31)
+    evac_all = n["s"]
 
     slot0 = [r for r in rem if am[r][1] == 0]
     slot1 = [r for r in rem if am[r][1] == 1]
     lord = [loc[(li + d) % nl] for d in range(1, nl)]
     order = slot0 + slot1 + lord + [me]
+
+    FB = [T.PB4, T.PB5, T.PB6, T.PB7, T.TP2, T.TP3, T.TP0, T.TP1]
+    fl = {}
+    pe.wait_ge(S.vs, n["v"])
+    for j, r in enumerate(order):
+        if j == 8:
+            pe.wait_ge(S.ss, evac_all)
+        h = 256 * (j % 2)
+        fl[j] = PE(pe.matmul(FB[j // 2][:, h:h + 256], T.ONESB[:], T.D[:, 256 * r:256 * r + 256], True, True))
+
     sc.wait_ge(S.ss, n["s"])
     sc.wait_ge(S.vs, ready[rb])
     gd = {}
@@ -324,13 +360,20 @@ def rank_program(g, core, T, topo):
 
     for j, r in enumerate(order):
         v.wait_ge(S.ss, gd[r])
-        sd[r] = V(v.tensor_tensor_scan(T.SC[:, 257 * r + 1:257 * r + 257], T.FL[:, 256 * r:256 * r + 256],
+        v.wait_ge(S.ps, fl[j | 1])
+        h = 256 * (j % 2)
+        sd[r] = V(v.tensor_tensor_scan(T.SC[:, 257 * r + 1:257 * r + 257], FB[j // 2][:, h:h + 256],
                                        T.G[:, 256 * r:256 * r + 256], 0.0, A.mult, A.add))
         if j:
             ends(order[j - 1])
     ends(order[-1])
 
     per_p = _pow2(len(eng_on) // 4)
+    cuts = [(0, 4), (4, 6), (6, nl - 1)]
+    perd = {}
+    for a, b in cuts:
+        for i in range(a, b):
+            perd[i + 1] = _pow2(len(eng_on) // (b - a))
 
     def to_agg(rs):
         g.wait_ge(S.vs, pd[rs[-1]])
@@ -341,11 +384,12 @@ def rank_program(g, core, T, topo):
         fused(trs)
         n["snt"] += per_p * len(trs)
 
-    def to_req(rs):
+    def to_req(a, b):
+        rs, per = lord[a:b], perd[a + 1]
         g.wait_ge(S.vs, pd[rs[-1]])
-        fused([RemoteDMATransfer(dst_ids=[did(cores[r])], dma_engine_mask=group(eng_on, j, per_p), remote_sem=S["rc%d" % li],
+        fused([RemoteDMATransfer(dst_ids=[did(cores[r])], dma_engine_mask=group(eng_on, j, per), remote_sem=S["rc%d" % li],
                                  src=T.P[:, 128 * r:128 * r + 128], dst=T.RECV[:, 128 * li:128 * li + 128]) for j, r in enumerate(rs)])
-        n["snt"] += per_p * len(rs)
+        n["snt"] += per * len(rs)
 
     def fold(s):
         for r in rem:
@@ -359,26 +403,27 @@ def rank_program(g, core, T, topo):
     to_agg(slot0)
     to_agg(slot1)
     fold(0)
-    to_req(lord[0:4])
     fold(1)
-    to_req(lord[4:])
+    for a, b in cuts:
+        to_req(a, b)
 
-    pe.wait_ge(S.ss, evac[4])
-    seq = [(li - d) % nl for d in range(1, 5)] + [-1] + [(li - d) % nl for d in range(5, nl)] + [-2]
-    for j, s in enumerate(seq):
-        if s == -1:
+    pe.wait_ge(S.vs, sd[order[1]])
+    seq = list(range(1, nl - 1)) + [-1, nl - 1, -2]
+    for j, d in enumerate(seq):
+        if d == -1:
             pe.wait_ge(S.vs, pd[me])
             src = T.P[:, 128 * me:128 * me + 128]
-        elif s == -2:
+        elif d == -2:
             pe.wait_ge(S.rx, len(eng_off))
             src = T.RX[:]
         else:
-            pe.wait_ge(S["rc%d" % s], per_p)
+            s = (li - d) % nl
+            pe.wait_ge(S["rc%d" % s], perd[d])
             src = T.RECV[:, 128 * s:128 * s + 128]
-        i = pe.matmul(T.TP0[:, 0:128], src, T.IDENT[:], j == 0, j == len(seq) - 1)
+        i = pe.matmul(T.PB4[:, 0:128], src, T.IDENT[:], j == 0, j == len(seq) - 1)
     k = PE(i)
     v.wait_ge(S.ps, k)
-    k = V(v.tensor_copy(T.YS[:], T.TP0[:, 0:128]))
+    k = V(v.tensor_copy(T.YS[:], T.PB4[:, 0:128]))
     g.sync.wait_ge(S.vs, k)
     g.sync.dma_start(T.y[:], T.YS[:]).then_inc(S.yd, 16)
 

@@ -16,6 +16,7 @@ SCRATCH = {
     "U1": ("sbuf", [128, 256], U16), "U2": ("sbuf", [128, 256], U16),
     "G": ("sbuf", [128, 4096], F32), "SC": ("sbuf", [128, 4112], F32),
     "P": ("sbuf", [128, 2048], F32), "AGG": ("sbuf", [128, 2048], F32), "RECV": ("sbuf", [128, 1024], F32),
+    "AGS": ("sbuf", [128, 256], F32), "ACC": ("sbuf", [128, 128], F32),
     "RX": ("sbuf", [128, 128], F32), "YS": ("sbuf", [128, 128], F32),
     "TABN": ("sbuf", [128, 4096], F32), "TABT": ("sbuf", [128, 4096], F32),
     "TP0": ("psum", [128, 512], F32), "TP1": ("psum", [128, 512], F32), "TP2": ("psum", [128, 512], F32),
@@ -391,39 +392,47 @@ def rank_program(g, core, T, topo):
                                  src=T.P[:, 128 * r:128 * r + 128], dst=T.RECV[:, 128 * li:128 * li + 128]) for j, r in enumerate(rs)])
         n["snt"] += per * len(rs)
 
-    def fold(s):
+    AB = [T.PB4, T.PB5]
+    ags = {}
+    for s in range(2):
         for r in rem:
             if am[r] == (core, s):
-                g.wait_ge(S["ag%d" % s], per_p * (nl - 1))
-                srcs = [T.AGG[:, 128 * (8 * s + j):128 * (8 * s + j) + 128] for j in range(nl) if j != li]
-                fused([RemoteDMATransfer(dst_ids=[did(cores[r])], dma_engine_mask=sum(eng_off), remote_sem=S.rx,
-                                         srcs=srcs + [T.P[:, 128 * r:128 * r + 128]], dsts=[T.RX[:]], alu_op=1)])
-                n["snt"] += len(eng_off)
+                pe.wait_ge(S.vs, max(sd[order[2 * s + 1]], pd[r]))
+                pe.wait_ge(S["ag%d" % s], per_p * (nl - 1))
+                for j in range(nl):
+                    src = T.P[:, 128 * r:128 * r + 128] if j == li else T.AGG[:, 128 * (8 * s + j):128 * (8 * s + j) + 128]
+                    i = pe.matmul(AB[s][:, 0:128], src, T.IDENT[:], j == 0, j == nl - 1)
+                k = PE(i)
+                sc.wait_ge(S.ps, k)
+                ags[s] = (r, SA(sc.activation(T.AGS[:, 128 * s:128 * s + 128], AB[s][:, 0:128], COPY)))
+
+    def send(s):
+        if s in ags:
+            r, k = ags[s]
+            g.wait_ge(S.ss, k)
+            fused([RemoteDMATransfer(dst_ids=[did(cores[r])], dma_engine_mask=sum(eng_off), remote_sem=S.rx,
+                                     src=T.AGS[:, 128 * s:128 * s + 128], dst=T.RX[:])])
+            n["snt"] += len(eng_off)
 
     to_agg(slot0)
     to_agg(slot1)
-    fold(0)
-    fold(1)
     for a, b in cuts:
         to_req(a, b)
+    send(0)
+    send(1)
 
-    pe.wait_ge(S.vs, sd[order[1]])
-    seq = list(range(1, nl - 1)) + [-1, nl - 1, -2]
-    for j, d in enumerate(seq):
-        if d == -1:
-            pe.wait_ge(S.vs, pd[me])
-            src = T.P[:, 128 * me:128 * me + 128]
-        elif d == -2:
-            pe.wait_ge(S.rx, len(eng_off))
-            src = T.RX[:]
-        else:
-            s = (li - d) % nl
-            pe.wait_ge(S["rc%d" % s], perd[d])
-            src = T.RECV[:, 128 * s:128 * s + 128]
-        i = pe.matmul(T.PB4[:, 0:128], src, T.IDENT[:], j == 0, j == len(seq) - 1)
-    k = PE(i)
+    for d in range(1, nl):
+        s = (li - d) % nl
+        v.wait_ge(S["rc%d" % s], perd[d])
+        vw()
+        k = V(v.tensor_tensor(T.ACC[:], T.P[:, 128 * me:128 * me + 128] if d == 1 else T.ACC[:],
+                              T.RECV[:, 128 * s:128 * s + 128], A.add))
+    pe.wait_ge(S.vs, k)
+    pe.matmul(T.PB6[:, 0:128], T.ACC[:], T.IDENT[:], True, False)
+    pe.wait_ge(S.rx, len(eng_off))
+    k = PE(pe.matmul(T.PB6[:, 0:128], T.IDENT[:], T.RX[:], False, True))
     v.wait_ge(S.ps, k)
-    k = V(v.tensor_copy(T.YS[:], T.PB4[:, 0:128]))
+    k = V(v.tensor_copy(T.YS[:], T.PB6[:, 0:128]))
     g.sync.wait_ge(S.vs, k)
     g.sync.dma_start(T.y[:], T.YS[:]).then_inc(S.yd, 16)
 

from concourse.bass import DstId, RemoteDMATransfer
from concourse.mybir import AluOpType, ActivationFunctionType

N = 16
F32, BF, I32, U16 = "float32", "bfloat16", "int32", "uint16"
SCRATCH = {
    "IDX": ("sbuf", [128, 8], I32), "IT": ("sbuf", [128, 64], I32), "FT": ("sbuf", [128, 128], F32),
    "ONESF": ("sbuf", [128, 128], F32), "IDENT": ("sbuf", [128, 128], F32), "ONESB": ("sbuf", [128, 128], BF),
    "LT": ("sbuf", [128, 128], BF), "CLT": ("sbuf", [128, 128], BF), "AT": ("sbuf", [128, 128], BF),
    "IOTAB": ("sbuf", [128, 128], BF), "EXP": ("sbuf", [128, 1024], BF), "BSEL": ("sbuf", [128, 128], BF),
    "SH": ("sbuf", [128, 129], BF), "D": ("sbuf", [128, 4096], BF),
    "OH": ("sbuf", [128, 128], BF), "TOTB": ("sbuf", [128, 128], BF), "SELM": ("sbuf", [128, 128], F32),
    "TR": ("sbuf", [128, 128], F32), "LH": ("sbuf", [128, 1024], BF), "RH": ("sbuf", [128, 512], BF),
    "MSG": ("sbuf", [128, 256], BF), "LAND": ("sbuf", [128, 256], BF), "RELAY": ("sbuf", [128, 128], BF),
    "HL": ("sbuf", [128, 64], BF), "TM": ("sbuf", [128, 256], F32), "TS": ("sbuf", [128, 256], F32),
    "U1": ("sbuf", [128, 256], U16), "U2": ("sbuf", [128, 256], U16),
    "G": ("sbuf", [128, 4096], F32), "SC": ("sbuf", [128, 4112], F32),
    "P": ("sbuf", [128, 2048], F32), "AGG": ("sbuf", [128, 2048], F32), "RECV": ("sbuf", [128, 1024], F32),
    "AGS": ("sbuf", [128, 256], F32), "ACC": ("sbuf", [128, 128], F32),
    "RX": ("sbuf", [128, 128], F32), "YS": ("sbuf", [128, 128], F32),
    "TABN": ("sbuf", [128, 4096], F32), "TABT": ("sbuf", [128, 4096], F32),
    "TP0": ("psum", [128, 512], F32), "TP1": ("psum", [128, 512], F32), "TP2": ("psum", [128, 512], F32),
    "TP3": ("psum", [128, 512], F32), "PB4": ("psum", [128, 512], F32), "PB5": ("psum", [128, 512], F32),
    "PB6": ("psum", [128, 512], F32), "PB7": ("psum", [128, 512], F32),
}
SEMAPHORES = (["vs", "ss", "ps", "gs", "ix", "ll", "lr", "rl", "snt", "ag0", "ag1", "rx", "yd"]
              + ["ta%d" % q for q in range(4)] + ["td%d" % q for q in range(1, 8)] + ["rc%d" % q for q in range(8)])


def _engines(m):
    out, b = [], 1
    while b <= m:
        if m & b:
            out.append(b)
        b <<= 1
    return out


def _pow2(n):
    p = 1
    while 2 * p <= n:
        p *= 2
    return p


def rank_program(g, core, T, topo):
    me = T.rank_of(core)
    if me is None:
        return
    A, S = AluOpType, T.sem
    COPY = ActivationFunctionType.Copy
    cores = list(T.cores)

    def same_chip(a, b):
        return topo.host(a) == topo.host(b) and topo.chip(a) == topo.chip(b)

    loc = [r for r in range(N) if same_chip(cores[r], core)]
    rem = [r for r in range(N) if not same_chip(cores[r], core)]
    li, nl = loc.index(me), len(loc)
    lb, rb = 16 * min(loc), 16 * min(rem)

    def ports_of(ranks, others):
        return [cores[r] for r in ranks if topo.may_write(cores[r], cores[others[0]])]

    def aggmap(ranks, others):
        ports, m = ports_of(ranks, others), {}
        for d in sorted(set(topo.die(p) for p in ports)):
            pd = [p for p in ports if topo.die(p) == d]
            qd = [r for r in others if topo.die(cores[r]) == d]
            for i, r in enumerate(qd):
                m[r] = (pd[i % len(pd)], i // len(pd))
        return m

    ports = ports_of(loc, rem)
    is_port = core in ports
    buddy = {}
    for d in sorted(set(topo.die(p) for p in ports)):
        pd = [p for p in ports if topo.die(p) == d]
        nd = [cores[r] for r in loc if topo.die(cores[r]) == d and cores[r] not in ports]
        for i, x in enumerate(nd):
            buddy[x] = pd[i % len(pd)]
    clients = [x for x in buddy if buddy[x] == core]
    am = aggmap(loc, rem)

    def did(c):
        rid, pid = topo.addr(c, core)
        return DstId(rid=rid, pnc=pid)

    n = {"v": 0, "s": 0, "p": 0, "g": 0, "snt": 0}

    def V(i):
        i.then_inc(S.vs, 1)
        n["v"] += 1
        return n["v"]

    def SA(i):
        i.then_inc(S.ss, 1)
        n["s"] += 1
        return n["s"]

    def PE(i):
        i.then_inc(S.ps, 1)
        n["p"] += 1
        return n["p"]

    def GC(i):
        i.then_inc(S.gs, 1)
        n["g"] += 1
        return n["g"]

    v, pe, sc = g.vector, g.tensor, g.scalar

    def vw():
        v.wait_ge(S.vs, n["v"])

    def it(k):
        return T.IT[:, 8 * k:8 * k + 8]

    def ft(k):
        return T.FT[:, 8 * k:8 * k + 8]

    g.sync.dma_start(T.IDX[:], T.idx[:]).then_inc(S.ix, 16)
    for t in range(4):
        (sc if t % 2 == 0 else g.sync).dma_start(T.TABN[:, 128 * t:128 * t + 128],
                                                 T.tab[128 * t:128 * t + 128, :]).then_inc(S["ta%d" % t], 16)
    for q in range(1, 8):
        (g.sync if q % 2 == 0 else sc).dma_start(T.TABN[:, 512 * q:512 * q + 512],
                                                 T.tab[512 * q:512 * q + 512, :]).then_inc(S["td%d" % q], 16)

    V(v.memset(T.ONESF[:], 1.0))
    V(v.memset(T.ONESB[:], 1.0))
    m1 = V(v.memset(T.AT[:], 256.0))
    V(v.memset(T.MSG[:], 0.0))
    V(v.memset(T.BSEL[:], 1.0))
    V(v.memset(T.SH[:], 1.0))
    V(v.memset(T.SC[:, 0:4112:257], 0.0))
    m2 = V(v.memset(T.EXP[:], 1.0))

    g.wait_ge(S.vs, m1)
    g_ident = GC(g.affine_select(T.IDENT[:], T.ONESF[:], [[-1, 128]], A.is_equal, 0.0, 0, 1))
    g_iota = GC(g.iota(T.IOTAB[:], [[1, 128]], 0, 0, allow_small_or_imprecise_dtypes=True))
    GC(g.affine_select(T.LT[:], T.ONESB[:], [[1, 128]], A.is_gt, 0.0, 0, -1))
    GC(g.affine_select(T.AT[:], T.AT[:], [[-1, 128]], A.is_gt, 0.0, 0, 1))
    g.wait_ge(S.gs, n["g"])
    GC(g.affine_select(T.CLT[:], T.LT[:], [[-8, 16], [0, 8]], A.is_ge, 0.0, 0, 1))
    g_rank = GC(g.affine_select(T.AT[:], T.AT[:], [[8, 16], [0, 8]], A.is_ge, 0.0, 7, -1))
    g.wait_ge(S.vs, m2)
    GC(g.affine_select(T.BSEL[:], T.BSEL[:], [[0, 8], [-8, 16]], A.is_ge, 0.0, 0, 1))
    g_sh = GC(g.affine_select(T.SH[:], T.SH[:], [[1, 129]], A.is_equal, 0.0, -1, -1))
    g.wait_ge(S.gs, n["g"])
    GC(g.affine_select(T.BSEL[:], T.BSEL[:], [[0, 8], [8, 16]], A.is_ge, 0.0, 7, -1))
    g_exp = GC(g.affine_select(T.EXP[:], T.EXP[:], [[-16, 8], [0, 8], [-1, 16]], A.is_equal, 0.0, 0, 1))

    TP = [T.TP0, T.TP1, T.TP2, T.TP3]
    evac = {}
    nxt = [0]

    def tiles(upto):
        while nxt[0] <= upto:
            k = nxt[0]
            nxt[0] += 1
            q, t = k // 4, k % 4
            if k == 0:
                pe.wait_ge(S.gs, g_ident)
            if q == 0:
                pe.wait_ge(S["ta%d" % t], 16)
            elif t == 0:
                pe.wait_ge(S["td%d" % q], 16)
            bank, col = TP[q % 4], 128 * t
            if k >= 30:
                bank, col = TP[k - 30], 0
                pe.wait_ge(S.ss, evac[k - 26])
            elif t == 0 and q >= 4:
                pe.wait_ge(S.ss, evac[q - 4])
            c = PE(pe.transpose(bank[:, col:col + 128], T.TABN[:, 128 * k:128 * k + 128], T.IDENT[:]))
            if q == 0:
                if t == 3:
                    sc.wait_ge(S.ps, c)
                    evac[0] = SA(sc.activation(T.TABT[:, 0:512], T.TP0[:, 0:512], COPY))
            elif q < 7:
                if t == 3:
                    sc.wait_ge(S.ps, c)
                    for u in range(4):
                        evac[q] = SA(sc.activation(T.TABT[:, 512 * q + u:512 * q + 512:4], bank[:, 128 * u:128 * u + 128], COPY))
            elif t == 1:
                sc.wait_ge(S.ps, c)
                for u in range(2):
                    SA(sc.activation(T.TABT[:, 512 * q + u:512 * q + 512:4], bank[:, 128 * u:128 * u + 128], COPY))
            elif t >= 2:
                sc.wait_ge(S.ps, c)
                evac[q] = SA(sc.activation(T.TABT[:, 512 * q + t:512 * q + 512:4], bank[:, 0:128], COPY))

    tiles(0)
    OWNI, HII, LOI, VPI, RKI, R7I = it(0), it(1), it(2), it(3), it(4), it(5)
    OWNF, OWN2, HIF, LOF, VP, NLF, ISL, NL4, RKF, R7F, HV, IHF, RK1, COLF, V2F = [ft(k) for k in range(15)]
    v.wait_ge(S.ix, 16)
    V(v.tensor_scalar(OWNI, T.IDX[:], 12, None, A.logical_shift_right))
    V(v.tensor_scalar(HII, T.IDX[:], 4032, None, A.bitwise_and))
    V(v.tensor_scalar(LOI, T.IDX[:], 63, None, A.bitwise_and))
    vw()
    V(v.tensor_copy(OWNF, OWNI))
    vw()
    v.wait_ge(S.gs, g_iota)
    for c in range(8):
        oh = V(v.tensor_scalar(T.OH[:, c:128:8], T.IOTAB[:, 0:16], OWNF[:, c:c + 1], None, A.is_equal))
    V(v.tensor_copy(HIF, HII))
    V(v.tensor_copy(LOF, LOI))
    V(v.tensor_scalar(OWN2, OWNF, 2.0, None, A.mult))
    pe.wait_ge(S.vs, oh)
    c = PE(pe.matmul(T.PB4[:, 0:128], T.OH[:], T.ONESB[:], True, True))
    tiles(1)
    v.wait_ge(S.ps, c)
    c = V(v.tensor_copy(T.TOTB[:], T.PB4[:, 0:128]))
    pe.wait_ge(S.vs, c)
    pe.wait_ge(S.gs, g_rank)
    pe.matmul(T.PB5[:, 0:128], T.LT[:], T.OH[:], True, False)
    pe.matmul(T.PB5[:, 0:128], T.AT[:], T.OH[:], False, False)
    c = PE(pe.matmul(T.PB5[:, 0:128], T.TOTB[:], T.CLT[:], False, True))
    tiles(5)
    v.wait_ge(S.ps, c)
    V(v.tensor_tensor(T.SELM[:], T.PB5[:, 0:128], T.OH[:], A.mult))
    vw()
    V(v.tensor_tensor(T.TR[:, 0:64], T.SELM[:, 0:64], T.SELM[:, 64:128], A.add))
    vw()
    V(v.tensor_tensor(T.TR[:, 64:96], T.TR[:, 0:32], T.TR[:, 32:64], A.add))
    vw()
    V(v.tensor_tensor(T.TR[:, 96:112], T.TR[:, 64:80], T.TR[:, 80:96], A.add))
    vw()
    V(v.tensor_tensor(VP, T.TR[:, 96:104], T.TR[:, 104:112], A.add))
    vw()
    V(v.tensor_copy(VPI, VP))
    V(v.tensor_scalar(NLF, VP, 256.0, None, A.is_ge))
    V(v.tensor_scalar(ISL, VP, 256.0, None, A.is_lt))
    vw()
    V(v.tensor_scalar(RKI, VPI, 255, None, A.bitwise_and))
    V(v.tensor_scalar(R7I, VPI, 127, None, A.bitwise_and))
    V(v.tensor_scalar(NL4, NLF, 4096.0, None, A.mult))
    vw()
    V(v.tensor_copy(RKF, RKI))
    V(v.tensor_copy(R7F, R7I))
    V(v.tensor_tensor(HV, NL4, HIF, A.add))
    vw()
    V(v.tensor_scalar(IHF, RKF, 128.0, None, A.is_ge))
    V(v.tensor_scalar(RK1, RKF, 1.0, None, A.add))
    vw()
    V(v.tensor_tensor(COLF, IHF, OWN2, A.add))
    V(v.tensor_tensor(V2F, RK1, ISL, A.mult))
    vw()
    for c in range(8):
        V(v.tensor_scalar(T.LH[:, 128 * c:128 * c + 128], T.IOTAB[:], R7F[:, c:c + 1], None, A.is_equal))
        V(v.tensor_scalar(T.RH[:, 64 * c:64 * c + 32], T.IOTAB[:, 0:32], COLF[:, c:c + 1], HV[:, c:c + 1], A.is_equal, A.mult))
        k = V(v.tensor_scalar(T.RH[:, 64 * c + 32:64 * c + 64], T.IOTAB[:, 0:32], COLF[:, c:c + 1], LOF[:, c:c + 1], A.is_equal, A.mult))
        pe.wait_ge(S.vs, k)
        i = pe.matmul(T.PB4[:, 128:192], T.LH[:, 128 * c:128 * c + 128], T.RH[:, 64 * c:64 * c + 64], c == 0, c == 7)
        if c == 7:
            k = PE(i)
        tiles(6 + c)
    for c in range(8):
        V(v.tensor_scalar(T.MSG[:, 4 + c:256:16], T.IOTAB[:, 0:16], OWNF[:, c:c + 1], V2F[:, c:c + 1], A.is_equal, A.mult))
    v.wait_ge(S.ps, k)
    for s in range(2):
        for ih in range(2):
            V(v.tensor_copy(T.MSG[:, 2 * s + ih:256:16], T.PB4[:, 128 + 32 * s + ih:128 + 32 * s + 32:2]))
    msg = n["v"]
    vw()
    V(v.tensor_copy(T.LAND[:, 16 * me:16 * me + 16], T.MSG[:, 16 * me:16 * me + 16]))

    def fused(trs):
        g.remote_dma_fused(trs, local_sem=S.snt)

    def group(engs, i, per):
        return sum(engs[i * per:(i + 1) * per])

    eng_on = _engines(topo.mask(core, cores[loc[(li + 1) % nl]]))
    eng_off = _engines(topo.mask(ports[0], cores[rem[0]]))
    per_l, per_r = _pow2(len(eng_on) // (nl - 1)), _pow2(len(eng_off) // len(rem))

    def cross(src, r):
        fused([RemoteDMATransfer(dst_ids=[did(cores[o])], dma_engine_mask=group(eng_off, j, per_r), remote_sem=S.lr,
                                 src=src[:, 16 * j:16 * j + 16], dst=T.LAND[:, 16 * r:16 * r + 16]) for j, o in enumerate(rem)])
        n["snt"] += per_r * len(rem)

    g.wait_ge(S.vs, msg)
    if is_port:
        cross(T.MSG[:, rb:rb + 128], me)
    else:
        rid, pid = topo.addr(buddy[core], core)
        g.remote_dma(T.RELAY[:], T.MSG[:, rb:rb + 128], S.rl, S.snt, pid, rid, topo.mask(core, buddy[core]))
        n["snt"] += len(eng_on)
    others = [r for r in loc if r != me]
    fused([RemoteDMATransfer(dst_ids=[did(cores[o])], dma_engine_mask=group(eng_on, j, per_l), remote_sem=S.ll,
                             src=T.MSG[:, 16 * o:16 * o + 16], dst=T.LAND[:, 16 * me:16 * me + 16]) for j, o in enumerate(others)])
    n["snt"] += per_l * len(others)
    for x in clients:
        g.wait_ge(S.rl, len(eng_on) * len(clients))
        cross(T.RELAY[:], T.rank_of(x))

    ready = {}

    def expand(cb, hh, ranks, sem, cnt):
        v.wait_ge(sem, cnt)
        vw()
        for s in range(2):
            for ih in range(2):
                k = V(v.tensor_copy(T.HL[:, 32 * hh + 16 * s + ih:32 * hh + 16 * s + 16:2], T.LAND[:, cb + 2 * s + ih:cb + 128:16]))
        pe.wait_ge(S.vs, k)
        pe.wait_ge(S.gs, g_exp)
        pb = 256 * hh
        for x in range(8):
            PE(pe.matmul(T.PB6[:, pb + x:pb + 256:8], T.EXP[:, 128 * x:128 * x + 128], T.HL[:, 32 * hh:32 * hh + 32], True, True))
        k = PE(pe.matmul(T.PB7[:, cb:cb + 128], T.BSEL[:], T.LAND[:, cb:cb + 128], True, True))
        v.wait_ge(S.gs, g_sh)
        for r in ranks:
            V(v.tensor_scalar(T.D[:, 256 * r:256 * r + 129], T.SH[:, 0:129], T.LAND[:, 16 * r:16 * r + 1], 4096.0, A.mult, A.is_ge))
            V(v.tensor_scalar(T.D[:, 256 * r + 129:256 * r + 256], T.SH[:, 1:128], T.LAND[:, 16 * r + 1:16 * r + 2], 4096.0,
                              A.mult, A.is_ge))
        v.wait_ge(S.ps, k)
        V(v.tensor_scalar(T.TM[:, cb:cb + 128], T.PB6[:, pb:pb + 128], 4096.0, -4096.0, A.is_ge, A.mult))
        V(v.tensor_copy(T.U2[:, cb:cb + 128], T.PB7[:, cb:cb + 128]))
        vw()
        V(v.tensor_tensor(T.TS[:, cb:cb + 128], T.PB6[:, pb:pb + 128], T.TM[:, cb:cb + 128], A.add))
        vw()
        V(v.tensor_tensor(T.TS[:, cb:cb + 128], T.PB6[:, pb + 128:pb + 256], T.TS[:, cb:cb + 128], A.add))
        vw()
        ready[cb] = V(v.tensor_copy(T.U1[:, cb:cb + 128], T.TS[:, cb:cb + 128]))

    tiles(21)
    expand(lb, 0, loc, S.ll, per_l * (nl - 1))
    tiles(28)
    pe.wait_ge(S.vs, ready[lb])
    expand(rb, 1, rem, S.lr, per_r * len(rem))
    tiles(31)
    evac_all = n["s"]

    slot0 = [r for r in rem if am[r][1] == 0]
    slot1 = [r for r in rem if am[r][1] == 1]
    lord = [loc[(li + d) % nl] for d in range(1, nl)]
    order = slot0 + slot1 + lord + [me]

    FB = [T.PB4, T.PB5, T.PB6, T.PB7, T.TP2, T.TP3, T.TP0, T.TP1]
    fl = {}
    pe.wait_ge(S.vs, n["v"])
    for j, r in enumerate(order):
        if j == 8:
            pe.wait_ge(S.ss, evac_all)
        h = 256 * (j % 2)
        fl[j] = PE(pe.matmul(FB[j // 2][:, h:h + 256], T.ONESB[:], T.D[:, 256 * r:256 * r + 256], True, True))

    sc.wait_ge(S.ss, n["s"])
    sc.wait_ge(S.vs, ready[rb])
    gd = {}
    for r in order:
        gd[r] = SA(sc.activation(T.G[:, 256 * r:256 * r + 256], T.TABT[:, 0:4096].indirect(T.U1[:, 16 * r:16 * r + 16]), COPY))
    vw()
    sd, pd = {}, {}

    def ends(r):
        v.wait_ge(S.vs, sd[r])
        pd[r] = V(v.tensor_copy(T.P[:, 128 * r:128 * r + 128],
                                T.SC[:, 257 * r:257 * r + 257].indirect(T.U2[:, 16 * r + 4:16 * r + 12])))

    for j, r in enumerate(order):
        v.wait_ge(S.ss, gd[r])
        v.wait_ge(S.ps, fl[j | 1])
        h = 256 * (j % 2)
        sd[r] = V(v.tensor_tensor_scan(T.SC[:, 257 * r + 1:257 * r + 257], FB[j // 2][:, h:h + 256],
                                       T.G[:, 256 * r:256 * r + 256], 0.0, A.mult, A.add))
        if j:
            ends(order[j - 1])
    ends(order[-1])

    per_p = _pow2(len(eng_on) // 4)
    cuts = [(0, 4), (4, 6), (6, nl - 1)]
    perd = {}
    for a, b in cuts:
        for i in range(a, b):
            perd[i + 1] = _pow2(len(eng_on) // (b - a))

    def to_agg(rs):
        g.wait_ge(S.vs, pd[rs[-1]])
        trs = [RemoteDMATransfer(dst_ids=[did(am[r][0])], dma_engine_mask=group(eng_on, j, per_p), remote_sem=S["ag%d" % am[r][1]],
                                 src=T.P[:, 128 * r:128 * r + 128],
                                 dst=T.AGG[:, 128 * (8 * am[r][1] + li):128 * (8 * am[r][1] + li) + 128])
               for j, r in enumerate(rs) if am[r][0] != core]
        fused(trs)
        n["snt"] += per_p * len(trs)

    def to_req(a, b):
        rs, per = lord[a:b], perd[a + 1]
        g.wait_ge(S.vs, pd[rs[-1]])
        fused([RemoteDMATransfer(dst_ids=[did(cores[r])], dma_engine_mask=group(eng_on, j, per), remote_sem=S["rc%d" % li],
                                 src=T.P[:, 128 * r:128 * r + 128], dst=T.RECV[:, 128 * li:128 * li + 128]) for j, r in enumerate(rs)])
        n["snt"] += per * len(rs)

    AB = [T.PB4, T.PB5]
    ags = {}
    for s in range(2):
        for r in rem:
            if am[r] == (core, s):
                pe.wait_ge(S.vs, max(sd[order[2 * s + 1]], pd[r]))
                pe.wait_ge(S["ag%d" % s], per_p * (nl - 1))
                for j in range(nl):
                    src = T.P[:, 128 * r:128 * r + 128] if j == li else T.AGG[:, 128 * (8 * s + j):128 * (8 * s + j) + 128]
                    i = pe.matmul(AB[s][:, 0:128], src, T.IDENT[:], j == 0, j == nl - 1)
                k = PE(i)
                sc.wait_ge(S.ps, k)
                ags[s] = (r, SA(sc.activation(T.AGS[:, 128 * s:128 * s + 128], AB[s][:, 0:128], COPY)))

    def send(s):
        if s in ags:
            r, k = ags[s]
            g.wait_ge(S.ss, k)
            fused([RemoteDMATransfer(dst_ids=[did(cores[r])], dma_engine_mask=sum(eng_off), remote_sem=S.rx,
                                     src=T.AGS[:, 128 * s:128 * s + 128], dst=T.RX[:])])
            n["snt"] += len(eng_off)

    to_agg(slot0)
    to_agg(slot1)
    for a, b in cuts:
        to_req(a, b)
    send(0)
    send(1)

    for d in range(1, nl):
        s = (li - d) % nl
        v.wait_ge(S["rc%d" % s], perd[d])
        vw()
        k = V(v.tensor_tensor(T.ACC[:], T.P[:, 128 * me:128 * me + 128] if d == 1 else T.ACC[:],
                              T.RECV[:, 128 * s:128 * s + 128], A.add))
    pe.wait_ge(S.vs, k)
    pe.matmul(T.PB6[:, 0:128], T.ACC[:], T.IDENT[:], True, False)
    pe.wait_ge(S.rx, len(eng_off))
    k = PE(pe.matmul(T.PB6[:, 0:128], T.IDENT[:], T.RX[:], False, True))
    v.wait_ge(S.ps, k)
    k = V(v.tensor_copy(T.YS[:], T.PB6[:, 0:128]))
    g.sync.wait_ge(S.vs, k)
    g.sync.dma_start(T.y[:], T.YS[:]).then_inc(S.yd, 16)

    g.wait_ge(S.yd, 16)
    g.wait_ge(S.vs, n["v"])
    g.wait_ge(S.ss, n["s"])
    g.wait_ge(S.ps, n["p"])
    g.wait_ge(S.gs, n["g"])
    g.wait_ge(S.snt, n["snt"])
